import numpy as np
import ml_dtypes


def mxq(x, axis, fmt="e4m3"):
    dtype, down = {"e4m3": (ml_dtypes.float8_e4m3fn, 7), "e5m2": (ml_dtypes.float8_e5m2, 14)}[fmt]
    v = np.moveaxis(np.asarray(x, np.float32).astype(ml_dtypes.bfloat16).astype(np.float64), axis, -1)
    blocks = v.reshape(v.shape[:-1] + (-1, 32))
    amax = np.abs(blocks).max(-1, keepdims=True)
    byte = np.maximum(np.where(amax > 0, np.frexp(amax)[1] - 1 + 127, 0) - down, 1)
    scale = np.exp2(byte - 127.0)
    codes = (blocks / scale).astype(np.float32).astype(dtype).astype(np.float64)
    return np.moveaxis((codes * scale).reshape(v.shape), -1, axis)


WIDE = False


def mx_kscale(k):
    if not WIDE:
        return np.ones(k)
    levels = np.array([10, -10, 5, -5, 0])
    if k % 512:
        return np.exp2(np.random.permutation(np.resize(levels, k // 32))).repeat(32)
    a = np.empty((k // 512, 16))
    for p in range(k // 512):
        a[p, :8] = np.random.permutation(np.resize(levels, 8))
        for g in range(8):
            far = levels[np.abs(levels - a[p, g]) >= 10]
            a[p, g + 8] = far[np.random.randint(len(far))]
    return np.exp2(a.ravel()).repeat(32)


def f64(x):
    return np.asarray(x).astype(np.float64)


def striped(idx):
    return np.tile(idx.reshape(-1, 16).T, (8, 1)).astype(np.uint16)


def unstriped(offs):
    return offs[:16].T.reshape(-1).astype(np.int64)


E2M1 = np.array([0.0, 0.5, 1.0, 1.5, 2.0, 3.0, 4.0, 6.0, -0.0, -0.5, -1.0, -1.5, -2.0, -3.0, -4.0, -6.0])


def pack_weight(w, fmt):
    k, n = w.shape
    w = f64(np.asarray(w, np.float32).astype(ml_dtypes.bfloat16)).reshape(k // 32, 32, n)
    amax = np.abs(w).max(1)
    if fmt == "e4m3":
        byte = np.frexp(amax)[1] - 1 + 127 - 7
    else:
        mant, ex = np.frexp(amax / 6.0)
        byte = np.where(mant > 0.5, ex, ex - 1) + 127
    byte = np.clip(np.where(amax > 0, byte, 1), 1, 254)
    scaled = (w * np.exp2(127.0 - byte)[:, None, :]).reshape(k, n).astype(np.float32)
    by_word = np.ascontiguousarray(scaled.reshape(k // 512, 128, 4, n).transpose(0, 1, 3, 2))
    if fmt == "e4m3":
        words = by_word.astype(ml_dtypes.float8_e4m3fn).view(np.uint8)
    else:
        c = by_word.astype(ml_dtypes.float4_e2m1fn).view(np.uint8) & 0xF
        words = (c[..., 0::2] | (c[..., 1::2] << 4)).reshape(k // 512, 128, 2 * n)
    return np.ascontiguousarray(words), np.ascontiguousarray(byte.astype(np.uint8).reshape(k // 512, 16, n))


def unpack_weight(words, scales, fmt):
    g, _, n = scales.shape
    words = np.ascontiguousarray(words).reshape(g, 128, n, -1)
    if fmt == "e4m3":
        vals = words.view(ml_dtypes.float8_e4m3fn).astype(np.float64)
    else:
        nib = np.empty((g, 128, n, 4), np.uint8)
        nib[..., 0::2] = words & 0xF
        nib[..., 1::2] = words >> 4
        vals = E2M1[nib]
    vals = vals * np.repeat(np.exp2(scales.astype(np.float64) - 127.0), 8, axis=1)[..., None]
    return vals.transpose(0, 1, 3, 2).reshape(g * 512, n)


def gelu(v):
    return 0.5 * v * (1.0 + np.tanh(np.sqrt(2.0 / np.pi) * (v + 0.044715 * v**3)))


def striped8(idx):
    return np.concatenate([v.reshape(-1, 16).T for v in idx]).astype(np.uint16)


def unstriped8(offs):
    return np.stack([offs[16 * g:16 * g + 16].T.reshape(-1) for g in range(8)]).astype(np.int64)


def heads(h, wgt, idx8):
    r = np.arange(h.shape[0])
    return wgt[r // 4 % 128] * h[r[:, None], idx8[r % 512 // 64]]


def put_heads(h, wgs, idx8, t2):
    r = np.arange(h.shape[0])
    page = np.zeros((h.shape[0], t2))
    page[r[:, None], idx8[r % 512 // 64]] = wgs[r // 4 % 128] * h
    return page


K, H, T, S, P, T2 = 1024, 1024, 4096, 1024, 512, 1024


def setup_inputs():
    n = np.random.standard_normal
    s = mx_kscale(K)[:, None]
    u = mx_kscale(H)[:, None]
    d = {}
    d["tab_words"], d["tab_scales"] = pack_weight(n((K, T)) * s, "e4m3")
    d["offs"] = striped(np.random.permutation(T)[:S])
    d["offs2"] = striped8(np.stack([np.random.permutation(S)[:P] for _ in range(8)]))
    d["offs3"] = striped8(np.stack([np.random.permutation(T2)[:P] for _ in range(8)]))
    d["w1"] = (n((K, H)) / s / K ** 0.5).astype(np.float32)
    d["w2_words"], d["w2_scales"] = pack_weight(n((K, H)) / s / K ** 0.5, "e2m1")
    d["gv"] = (np.exp(0.5 * n(H)) * u[:, 0]).astype(np.float32)
    d["w4"] = (n((H, H)) / u / H ** 0.5).astype(np.float32)
    d["gm"] = n((H, P)).astype(np.float32)
    d["wgt"] = np.repeat(np.random.uniform(0.5, 2.0, (8, P)), 16, axis=0).astype(np.float32)
    d["wgo"] = np.repeat(np.random.uniform(0.5, 2.0, (8, P)), 16, axis=0).astype(np.float32)
    return d


def reference(tab_words, tab_scales, offs, offs2, offs3, w1, w2_words, w2_scales, gv, w4, gm, wgt, wgo):
    v = unpack_weight(tab_words, tab_scales, "e4m3")[:, unstriped(offs)]
    a = mxq(f64(w1), 0, "e4m3").T @ v
    b = unpack_weight(w2_words, w2_scales, "e2m1").T @ v
    h = np.maximum(a, np.abs(b)) - b
    read = heads(h, f64(wgt), unstriped8(offs2))
    x = read * f64(gv)[:, None]
    mix = mxq(f64(w4), 0, "e4m3").T @ mxq(x, 0, "e4m3")
    y = mix * f64(gm) + read
    return put_heads(y, f64(wgo), unstriped8(offs3), T2)

@@ -1,0 +1,259 @@
+from contextlib import ExitStack
+
+import concourse.mybir as mybir
+
+K, H, T, S, M, T2 = 1024, 1024, 4096, 1024, 512, 1024
+FLOPS = 2 * K * H * S * 2 + 2 * H * H * M
+
+F32 = mybir.dt.float32
+BF16 = mybir.dt.bfloat16
+I32 = mybir.dt.int32
+U32 = mybir.dt.uint32
+U16 = mybir.dt.uint16
+U8 = mybir.dt.uint8
+FP8X4 = mybir.dt.float8_e4m3fn_x4
+FP4X4 = mybir.dt.float4_e2m1fn_x4
+ALU = mybir.AluOpType
+ACT = mybir.ActivationFunctionType
+
+P = 128
+PACK = 4
+PASS = P * PACK
+PASSES = K // PASS
+BLOCKS = H // PASS
+TILES = BLOCKS * PACK
+BANK = 512
+HALVES = S // BANK
+
+
+def tile_list_shade_chart_scores_kernel(
+    tc, tab_words, tab_scales, offs, offs2, offs3, w1, w2_words, w2_scales, gv, w4, gm, wgt, wgo, out
+):
+    nc = tc.nc
+    with ExitStack() as ctx:
+        keep = ctx.enter_context(tc.tile_pool(name="keep", bufs=1))
+        shared = ctx.enter_context(tc.tile_pool(name="shared", bufs=1))
+        early = ctx.enter_context(tc.tile_pool(name="early", bufs=1))
+        raws = ctx.enter_context(tc.tile_pool(name="raws", bufs=4))
+        ring = ctx.enter_context(tc.tile_pool(name="ring", bufs=3))
+        psum1 = ctx.enter_context(tc.psum_pool(name="psum1", bufs=3))
+        psum2 = ctx.enter_context(tc.psum_pool(name="psum2", bufs=2))
+
+        list1 = keep.tile([P, S // 16], U16, name="list1")
+        list2 = keep.tile([P, M // 16], U16, name="list2")
+        list3 = keep.tile([P, M // 16], U16, name="list3")
+
+        table = [shared.tile([P, T], U32, name=f"table{a}", offset=4 * T * a) for a in range(PASSES)]
+        table_sc = early.tile([P, PASSES, T], U8, name="table_sc", align_bytes=64, offset=0)
+        w2_raw = keep.tile([P, PASSES, 2 * H], U8, name="w2_raw", align_bytes=64)
+        w2_raw_sc = early.tile([P, PASSES, H], U8, name="w2_raw_sc", align_bytes=64, offset=PASSES * T)
+        w2_q = keep.tile([P, PASSES, 2 * H], U8, name="w2_q", align_bytes=64)
+        w2_sc = keep.tile([P, PASSES, H], U8, name="w2_sc", align_bytes=64)
+        gv_sb = keep.tile([P, BLOCKS, PACK], F32, name="gv_sb")
+        gm_sb = keep.tile([P, BLOCKS, PACK * M], F32, name="gm_sb")
+        wgt_sb = keep.tile([P, M], F32, name="wgt_sb")
+        wgo_sb = keep.tile([P, M], F32, name="wgo_sb")
+
+        nc.vector.memset(table_sc[:].rearrange("p a t -> p (a t)").bitcast(I32), 0)
+        nc.vector.memset(w2_raw_sc[:].rearrange("p a c -> p (a c)").bitcast(I32), 0)
+        for dst, src in ((table_sc, tab_scales), (w2_raw_sc, w2_scales)):
+            for q in range(4):
+                nc.gpsimd.dma_start(
+                    dst[32 * q : 32 * q + 4].bitcast(I32),
+                    src[:, 4 * q : 4 * q + 4, :].rearrange("a q c -> q a c").bitcast(I32),
+                )
+
+        raw = {}
+
+        def load_weight(w, key, a, b):
+            raw[key, a, b] = raws.tile([P, PACK, PASS], F32, name="raw")
+            rows = w[PASS * a : PASS * (a + 1), PASS * b : PASS * (b + 1)]
+            nc.sync.dma_start(raw[key, a, b][:], rows.rearrange("(p j) c -> p j c", j=PACK))
+
+        staged = {}
+        codes = {}
+        scales = {}
+
+        def weave_weight(key, a, b, part):
+            if part == 0:
+                staged[key, a, b] = ring.tile([P, PASS * PACK], BF16, name="staged", align_bytes=64)
+            ms = slice(64 * part, 64 * (part + 1))
+            nc.scalar.activation(
+                out=staged[key, a, b][:].rearrange("p (t m j) -> p m j t", t=PACK, j=PACK)[:, ms],
+                in_=raw[key, a, b][:].rearrange("p j (m t) -> p m j t", t=PACK)[:, ms],
+                func=ACT.Copy,
+            )
+
+        def quantise(key, a, b):
+            codes[key, a, b] = keep.tile([P, PASS], U32, name=f"codes_{key}{a}{b}", align_bytes=64)
+            scales[key, a, b] = keep.tile([P, PASS], U8, name=f"scales_{key}{a}{b}", align_bytes=64)
+            nc.vector.quantize_mx(
+                out=codes[key, a, b][:].bitcast(FP8X4), scales=scales[key, a, b][:], in_=staged[key, a, b][:]
+            )
+
+        nc.sync.dma_start(list1[:], offs)
+        load_weight(w1, "w1", 0, 0)
+        nc.sync.dma_start(w2_raw[:].bitcast(I32), w2_words.rearrange("a p c -> p a c").bitcast(I32))
+        load_weight(w1, "w1", 1, 0)
+        for a in range(PASSES):
+            nc.sync.dma_start(table[a][:].bitcast(I32), tab_words[a].rearrange("p t i -> p (t i)").bitcast(I32))
+        nc.sync.dma_start(list2[:], offs2)
+        nc.sync.dma_start(wgt_sb[:], wgt)
+        nc.sync.dma_start(gv_sb[:], gv.rearrange("(b p i) -> p b i", p=P, i=PACK))
+        load_weight(w1, "w1", 0, 1)
+        load_weight(w1, "w1", 1, 1)
+
+        for a in range(PASSES):
+            weave_weight("w1", a, 0, 0)
+            weave_weight("w1", a, 0, 1)
+        load_weight(w4, "w4", 0, 0)
+        load_weight(w4, "w4", 1, 0)
+        nc.sync.dma_start(gm_sb[:], gm.rearrange("(b p i) m -> p b (i m)", p=P, i=PACK))
+        nc.sync.dma_start(list3[:], offs3)
+        nc.sync.dma_start(wgo_sb[:], wgo)
+
+        nc.vector.tensor_copy(
+            out=w2_q[:].rearrange("p a c -> p (a c)").bitcast(U16).rearrange("p (g t m) -> p g t m", t=PACK, m=P),
+            in_=w2_raw[:].rearrange("p a c -> p (a c)").bitcast(U16).rearrange("p (g m t) -> p g t m", t=PACK, m=P),
+        )
+        v_sc = []
+        for a in range(PASSES):
+            v_sc.append(keep.tile([P, S], U8, name=f"v_sc{a}", align_bytes=64))
+            nc.vector.tensor_copy(v_sc[a][:], table_sc[:, a, :].indirect(list1[:]))
+            quantise("w1", a, 0)
+        nc.vector.tensor_copy(
+            out=w2_sc[:].rearrange("p a (b t m) -> p (a b) t m", t=PACK, m=P),
+            in_=w2_raw_sc[:].rearrange("p a (b m t) -> p (a b) t m", t=PACK, m=P),
+        )
+        v_q = {}
+        for a in range(PASSES):
+            for c in range(HALVES):
+                place = PASSES * T if (a, c) == (1, 0) else 4 * BANK * (HALVES * a + c)
+                v_q[a, c] = early.tile([P, BANK], U32, name=f"v_q{a}{c}", align_bytes=64, offset=place)
+                piece = list1[:, BANK // 16 * c : BANK // 16 * (c + 1)]
+                nc.vector.tensor_copy(v_q[a, c][:], table[a][:].indirect(piece))
+
+        pages = []
+        for n in range(TILES):
+            pages.append(shared.tile([P, T2], F32, name=f"page{n}", offset=4 * T2 * n))
+            nc.gpsimd.memset(pages[n][:], 0.0)
+
+        reads = []
+        x_planes = [keep.tile([P, PACK, M], BF16, name=f"x_planes{b}", align_bytes=64) for b in range(BLOCKS)]
+        h_tiles = []
+
+        def products(n):
+            b, i = divmod(n, PACK)
+            banks = []
+            for c in range(HALVES):
+                cols = slice(BANK * c, BANK * (c + 1))
+                pb = psum1.tile([P, BANK], F32, name="pb")
+                pa = psum1.tile([P, BANK], F32, name="pa")
+                for a in range(PASSES):
+                    nc.tensor.matmul_mx(
+                        out=pb[:],
+                        lhsT=w2_q[:, a, 2 * P * n : 2 * P * (n + 1)].bitcast(FP4X4),
+                        lhsT_scale=w2_sc[:, a, P * n : P * (n + 1)],
+                        rhs=v_q[a, c][:].bitcast(FP8X4),
+                        rhs_scale=v_sc[a][:, cols],
+                        start=(a == 0),
+                        stop=(a == PASSES - 1),
+                    )
+                for a in range(PASSES):
+                    nc.tensor.matmul_mx(
+                        out=pa[:],
+                        lhsT=codes["w1", a, b][:, P * i : P * (i + 1)].bitcast(FP8X4),
+                        lhsT_scale=scales["w1", a, b][:, P * i : P * (i + 1)],
+                        rhs=v_q[a, c][:].bitcast(FP8X4),
+                        rhs_scale=v_sc[a][:, cols],
+                        start=(a == 0),
+                        stop=(a == PASSES - 1),
+                    )
+                size_b = ring.tile([P, BANK], F32, name="size_b")
+                nc.scalar.activation(out=size_b[:], in_=pb[:], func=ACT.Abs)
+                top = ring.tile([P, BANK], F32, name="top")
+                nc.vector.tensor_tensor(top[:], pa[:], size_b[:], ALU.max)
+                banks.append((top, pb))
+            return banks
+
+        def differences(n, banks):
+            h_tiles.append(ring.tile([P, S], F32, name="h"))
+            for c, (top, pb) in enumerate(banks):
+                nc.vector.tensor_tensor(h_tiles[n][:, BANK * c : BANK * (c + 1)], top[:], pb[:], ALU.subtract)
+
+        def pick(n):
+            b, i = divmod(n, PACK)
+            reads.append(keep.tile([P, M], F32, name=f"read{n}"))
+            nc.vector.tensor_tensor(reads[n][:], h_tiles[n][:].indirect(list2[:]), wgt_sb[:], ALU.mult)
+            nc.scalar.activation(out=x_planes[b][:, i, :], in_=reads[n][:], func=ACT.Copy, scale=gv_sb[:, b, i : i + 1])
+
+        def weave_x(b, copy):
+            staged["x", b, 0] = ring.tile([P, M * PACK], BF16, name="staged", align_bytes=64)
+            copy(
+                out=staged["x", b, 0][:].rearrange("p (c e i) -> p c i e", e=4, i=PACK),
+                in_=x_planes[b][:].rearrange("p i (c e) -> p c i e", e=4),
+            )
+
+        for n in range(TILES):
+            banks = products(n)
+            if n > 0:
+                pick(n - 1)
+            differences(n, banks)
+            if n in (1, 2):
+                weave_weight("w1", n - 1, 1, 0)
+                weave_weight("w1", n - 1, 1, 1)
+                quantise("w1", n - 1, 1)
+                load_weight(w4, "w4", n - 1, 1)
+            if n in (3, 5):
+                weave_weight("w4", (n - 3) // 2, 0, 0)
+                weave_weight("w4", (n - 3) // 2, 0, 1)
+                quantise("w4", (n - 3) // 2, 0)
+            if n == 4:
+                weave_x(0, nc.scalar.copy)
+                quantise("x", 0, 0)
+            if n in (6, 7):
+                weave_weight("w4", n - 6, 1, 0)
+                weave_weight("w4", n - 6, 1, 1)
+        pick(TILES - 1)
+        quantise("w4", 0, 1)
+        weave_x(1, nc.vector.tensor_copy)
+        quantise("w4", 1, 1)
+        quantise("x", 1, 0)
+
+        out_rows = out.rearrange("(b p i) t -> b i p t", p=P, i=PACK)
+        gated = []
+        scores = []
+
+        def mix(n):
+            b, i = divmod(n, PACK)
+            bank = psum2.tile([P, M], F32, name="mix")
+            for a in range(BLOCKS):
+                nc.tensor.matmul_mx(
+                    out=bank[:],
+                    lhsT=codes["w4", a, b][:, P * i : P * (i + 1)].bitcast(FP8X4),
+                    lhsT_scale=scales["w4", a, b][:, P * i : P * (i + 1)],
+                    rhs=codes["x", a, 0][:].bitcast(FP8X4),
+                    rhs_scale=scales["x", a, 0][:],
+                    start=(a == 0),
+                    stop=(a == BLOCKS - 1),
+                )
+            gated.append(ring.tile([P, M], F32, name="gated"))
+            nc.vector.tensor_tensor(gated[n][:], bank[:], gm_sb[:, b, M * i : M * (i + 1)], ALU.mult)
+
+        def score(n):
+            scores.append(ring.tile([P, M], F32, name="score"))
+            nc.vector.tensor_tensor(scores[n][:], gated[n][:], reads[n][:], ALU.add)
+
+        def file_scores(n):
+            b, i = divmod(n, PACK)
+            nc.vector.tensor_tensor(pages[n][:].indirect(list3[:]), scores[n][:], wgo_sb[:], ALU.mult)
+            nc.sync.dma_start(out_rows[b, i], pages[n][:])
+
+        mix(0)
+        for n in range(TILES):
+            if n + 1 < TILES:
+                mix(n + 1)
+            score(n)
+            if n > 0:
+                file_scores(n - 1)
+        file_scores(TILES - 1)

@@ -50,39 +50,40 @@ def tile_list_shade_chart_scores_kernel(
         w2_q = keep.tile([P, PASSES, 2 * H], U8, name="w2_q", align_bytes=64)
         w2_sc = keep.tile([P, PASSES, H], U8, name="w2_sc", align_bytes=64)
         gv_sb = keep.tile([P, BLOCKS, PACK], F32, name="gv_sb")
-        gm_sb = keep.tile([P, BLOCKS, PACK * M], F32, name="gm_sb")
+        gm_sb = shared.tile([P, BLOCKS, PACK * M], F32, name="gm_sb", offset=0)
         wgt_sb = keep.tile([P, M], F32, name="wgt_sb")
         wgo_sb = keep.tile([P, M], F32, name="wgo_sb")
 
-        nc.vector.memset(table_sc[:].rearrange("p a t -> p (a t)").bitcast(I32), 0)
+        nc.gpsimd.memset(table_sc[:, 0, :].bitcast(I32), 0)
+        nc.vector.memset(table_sc[:, 1, :].bitcast(I32), 0)
         nc.vector.memset(w2_raw_sc[:].rearrange("p a c -> p (a c)").bitcast(I32), 0)
-        for dst, src in ((table_sc, tab_scales), (w2_raw_sc, w2_scales)):
-            for q in range(4):
-                nc.gpsimd.dma_start(
-                    dst[32 * q : 32 * q + 4].bitcast(I32),
-                    src[:, 4 * q : 4 * q + 4, :].rearrange("a q c -> q a c").bitcast(I32),
-                )
+        pages = []
+        for n in range(TILES):
+            pages.append(keep.tile([P, T2], F32, name=f"page{n}"))
+            nc.vector.memset(pages[n][:].bitcast(I32), 0)
 
         raw = {}
 
-        def load_weight(w, key, a, b):
+        def load_weight(w, key, a, b, pieces=1):
             raw[key, a, b] = raws.tile([P, PACK, PASS], F32, name="raw")
-            rows = w[PASS * a : PASS * (a + 1), PASS * b : PASS * (b + 1)]
-            nc.sync.dma_start(raw[key, a, b][:], rows.rearrange("(p j) c -> p j c", j=PACK))
+            rows = w[PASS * a : PASS * (a + 1), PASS * b : PASS * (b + 1)].rearrange("(p j) c -> p j c", j=PACK)
+            for e in range(pieces):
+                js = slice(PACK // pieces * e, PACK // pieces * (e + 1))
+                nc.sync.dma_start(raw[key, a, b][:, js, :], rows[:, js, :])
 
         staged = {}
         codes = {}
         scales = {}
 
-        def weave_weight(key, a, b, part):
-            if part == 0:
-                staged[key, a, b] = ring.tile([P, PASS * PACK], BF16, name="staged", align_bytes=64)
-            ms = slice(64 * part, 64 * (part + 1))
-            nc.scalar.activation(
-                out=staged[key, a, b][:].rearrange("p (t m j) -> p m j t", t=PACK, j=PACK)[:, ms],
-                in_=raw[key, a, b][:].rearrange("p j (m t) -> p m j t", t=PACK)[:, ms],
-                func=ACT.Copy,
-            )
+        def weave_weight(key, a, b, pool=ring):
+            staged[key, a, b] = pool.tile([P, PASS * PACK], BF16, name="staged", align_bytes=64)
+            for part in range(2):
+                ms = slice(64 * part, 64 * (part + 1))
+                nc.scalar.activation(
+                    out=staged[key, a, b][:].rearrange("p (t m j) -> p m j t", t=PACK, j=PACK)[:, ms],
+                    in_=raw[key, a, b][:].rearrange("p j (m t) -> p m j t", t=PACK)[:, ms],
+                    func=ACT.Copy,
+                )
 
         def quantise(key, a, b):
             codes[key, a, b] = keep.tile([P, PASS], U32, name=f"codes_{key}{a}{b}", align_bytes=64)
@@ -92,34 +93,45 @@ def tile_list_shade_chart_scores_kernel(
             )
 
         nc.sync.dma_start(list1[:], offs)
-        load_weight(w1, "w1", 0, 0)
+        nc.sync.dma_start(list2[:], offs2)
+        nc.sync.dma_start(list3[:], offs3)
+        nc.sync.dma_start(gv_sb[:], gv.rearrange("(b p i) -> p b i", p=P, i=PACK))
+        nc.sync.dma_start(wgt_sb[:], wgt)
+        load_weight(w1, "w1", 0, 0, 4)
+
+        def load_scale_rows(dst, src):
+            for q in range(4):
+                nc.sync.dma_start(
+                    dst[32 * q : 32 * q + 4].bitcast(I32),
+                    src[:, 4 * q : 4 * q + 4, :].rearrange("a q c -> q a c").bitcast(I32),
+                )
+
+        def load_table(a):
+            nc.sync.dma_start(table[a][:].bitcast(I32), tab_words[a].rearrange("p t i -> p (t i)").bitcast(I32))
+
+        load_scale_rows(table_sc, tab_scales)
         nc.sync.dma_start(w2_raw[:].bitcast(I32), w2_words.rearrange("a p c -> p a c").bitcast(I32))
         load_weight(w1, "w1", 1, 0)
-        for a in range(PASSES):
-            nc.sync.dma_start(table[a][:].bitcast(I32), tab_words[a].rearrange("p t i -> p (t i)").bitcast(I32))
-        nc.sync.dma_start(list2[:], offs2)
-        nc.sync.dma_start(wgt_sb[:], wgt)
-        nc.sync.dma_start(gv_sb[:], gv.rearrange("(b p i) -> p b i", p=P, i=PACK))
+        load_table(0)
+        load_scale_rows(w2_raw_sc, w2_scales)
+        load_table(1)
         load_weight(w1, "w1", 0, 1)
         load_weight(w1, "w1", 1, 1)
 
         for a in range(PASSES):
-            weave_weight("w1", a, 0, 0)
-            weave_weight("w1", a, 0, 1)
+            weave_weight("w1", a, 0)
         load_weight(w4, "w4", 0, 0)
         load_weight(w4, "w4", 1, 0)
-        nc.sync.dma_start(gm_sb[:], gm.rearrange("(b p i) m -> p b (i m)", p=P, i=PACK))
-        nc.sync.dma_start(list3[:], offs3)
-        nc.sync.dma_start(wgo_sb[:], wgo)
 
-        nc.vector.tensor_copy(
-            out=w2_q[:].rearrange("p a c -> p (a c)").bitcast(U16).rearrange("p (g t m) -> p g t m", t=PACK, m=P),
-            in_=w2_raw[:].rearrange("p a c -> p (a c)").bitcast(U16).rearrange("p (g m t) -> p g t m", t=PACK, m=P),
-        )
         v_sc = []
         for a in range(PASSES):
             v_sc.append(keep.tile([P, S], U8, name=f"v_sc{a}", align_bytes=64))
             nc.vector.tensor_copy(v_sc[a][:], table_sc[:, a, :].indirect(list1[:]))
+        nc.vector.tensor_copy(
+            out=w2_q[:].rearrange("p a c -> p (a c)").bitcast(U16).rearrange("p (g t m) -> p g t m", t=PACK, m=P),
+            in_=w2_raw[:].rearrange("p a c -> p (a c)").bitcast(U16).rearrange("p (g m t) -> p g t m", t=PACK, m=P),
+        )
+        for a in range(PASSES):
             quantise("w1", a, 0)
         nc.vector.tensor_copy(
             out=w2_sc[:].rearrange("p a (b t m) -> p (a b) t m", t=PACK, m=P),
@@ -133,10 +145,8 @@ def tile_list_shade_chart_scores_kernel(
                 piece = list1[:, BANK // 16 * c : BANK // 16 * (c + 1)]
                 nc.vector.tensor_copy(v_q[a, c][:], table[a][:].indirect(piece))
 
-        pages = []
-        for n in range(TILES):
-            pages.append(shared.tile([P, T2], F32, name=f"page{n}", offset=4 * T2 * n))
-            nc.gpsimd.memset(pages[n][:], 0.0)
+        nc.sync.dma_start(gm_sb[:], gm.rearrange("(b p i) m -> p b (i m)", p=P, i=PACK))
+        nc.sync.dma_start(wgo_sb[:], wgo)
 
         reads = []
         x_planes = [keep.tile([P, PACK, M], BF16, name=f"x_planes{b}", align_bytes=64) for b in range(BLOCKS)]
@@ -181,18 +191,25 @@ def tile_list_shade_chart_scores_kernel(
             for c, (top, pb) in enumerate(banks):
                 nc.vector.tensor_tensor(h_tiles[n][:, BANK * c : BANK * (c + 1)], top[:], pb[:], ALU.subtract)
 
-        def pick(n):
+        def pick(n, pieces=1):
             b, i = divmod(n, PACK)
             reads.append(keep.tile([P, M], F32, name=f"read{n}"))
-            nc.vector.tensor_tensor(reads[n][:], h_tiles[n][:].indirect(list2[:]), wgt_sb[:], ALU.mult)
-            nc.scalar.activation(out=x_planes[b][:, i, :], in_=reads[n][:], func=ACT.Copy, scale=gv_sb[:, b, i : i + 1])
+            for e in range(pieces):
+                ms = slice(M // pieces * e, M // pieces * (e + 1))
+                entries = list2[:, M // 16 // pieces * e : M // 16 // pieces * (e + 1)]
+                nc.vector.tensor_tensor(reads[n][:, ms], h_tiles[n][:].indirect(entries), wgt_sb[:, ms], ALU.mult)
+                nc.scalar.activation(
+                    out=x_planes[b][:, i, ms], in_=reads[n][:, ms], func=ACT.Copy, scale=gv_sb[:, b, i : i + 1]
+                )
 
-        def weave_x(b, copy):
-            staged["x", b, 0] = ring.tile([P, M * PACK], BF16, name="staged", align_bytes=64)
-            copy(
-                out=staged["x", b, 0][:].rearrange("p (c e i) -> p c i e", e=4, i=PACK),
-                in_=x_planes[b][:].rearrange("p i (c e) -> p c i e", e=4),
-            )
+        def weave_x(b, copy, pieces, pool=ring):
+            staged["x", b, 0] = pool.tile([P, M * PACK], BF16, name="staged", align_bytes=64)
+            for e in range(pieces):
+                cs = slice(M // 4 // pieces * e, M // 4 // pieces * (e + 1))
+                copy(
+                    out=staged["x", b, 0][:].rearrange("p (c e i) -> p c i e", e=4, i=PACK)[:, cs],
+                    in_=x_planes[b][:].rearrange("p i (c e) -> p c i e", e=4)[:, cs],
+                )
 
         for n in range(TILES):
             banks = products(n)
@@ -200,28 +217,20 @@ def tile_list_shade_chart_scores_kernel(
                 pick(n - 1)
             differences(n, banks)
             if n in (1, 2):
-                weave_weight("w1", n - 1, 1, 0)
-                weave_weight("w1", n - 1, 1, 1)
+                weave_weight("w1", n - 1, 1)
                 quantise("w1", n - 1, 1)
                 load_weight(w4, "w4", n - 1, 1)
             if n in (3, 5):
-                weave_weight("w4", (n - 3) // 2, 0, 0)
-                weave_weight("w4", (n - 3) // 2, 0, 1)
+                weave_weight("w4", (n - 3) // 2, 0)
                 quantise("w4", (n - 3) // 2, 0)
             if n == 4:
-                weave_x(0, nc.scalar.copy)
+                weave_x(0, nc.scalar.copy, 2)
                 quantise("x", 0, 0)
-            if n in (6, 7):
-                weave_weight("w4", n - 6, 1, 0)
-                weave_weight("w4", n - 6, 1, 1)
-        pick(TILES - 1)
-        quantise("w4", 0, 1)
-        weave_x(1, nc.vector.tensor_copy)
-        quantise("w4", 1, 1)
+        pick(TILES - 1, 2)
+        weave_x(1, nc.vector.tensor_copy, 2, keep)
         quantise("x", 1, 0)
 
         out_rows = out.rearrange("(b p i) t -> b i p t", p=P, i=PACK)
-        gated = []
         scores = []
 
         def mix(n):
@@ -237,23 +246,31 @@ def tile_list_shade_chart_scores_kernel(
                     start=(a == 0),
                     stop=(a == BLOCKS - 1),
                 )
-            gated.append(ring.tile([P, M], F32, name="gated"))
-            nc.vector.tensor_tensor(gated[n][:], bank[:], gm_sb[:, b, M * i : M * (i + 1)], ALU.mult)
-
-        def score(n):
-            scores.append(ring.tile([P, M], F32, name="score"))
-            nc.vector.tensor_tensor(scores[n][:], gated[n][:], reads[n][:], ALU.add)
+            gate = gm_sb[:, b, M * i : M * (i + 1)]
+            gated = ring.tile([P, M], F32, name="size_b")
+            if n == 0:
+                engine = nc.vector
+                nc.vector.tensor_tensor(gated[:], bank[:], gate, ALU.mult)
+            else:
+                engine = nc.gpsimd
+                mixed = ring.tile([P, M], F32, name="top")
+                nc.scalar.copy(mixed[:], bank[:])
+                nc.gpsimd.tensor_tensor(gated[:], mixed[:], gate, ALU.mult)
+            score = ring.tile([P, M], F32, name="score")
+            engine.tensor_tensor(score[:], gated[:], reads[n][:], ALU.add)
+            scores.append(ring.tile([P, M], F32, name="weighted"))
+            engine.tensor_tensor(scores[n][:], score[:], wgo_sb[:], ALU.mult)
 
         def file_scores(n):
             b, i = divmod(n, PACK)
-            nc.vector.tensor_tensor(pages[n][:].indirect(list3[:]), scores[n][:], wgo_sb[:], ALU.mult)
+            nc.vector.tensor_copy(pages[n][:].indirect(list3[:]), scores[n][:])
             nc.sync.dma_start(out_rows[b, i], pages[n][:])
 
         mix(0)
         for n in range(TILES):
+            if n < BLOCKS:
+                weave_weight("w4", n, 1, keep)
+                quantise("w4", n, 1)
             if n + 1 < TILES:
                 mix(n + 1)
-            score(n)
-            if n > 0:
-                file_scores(n - 1)
-        file_scores(TILES - 1)
+            file_scores(n)

@@ -1,6 +1,7 @@
 from contextlib import ExitStack
 
 import concourse.mybir as mybir
+from concourse.masks import make_identity
 
 K, H, T, S, M, T2 = 1024, 1024, 4096, 1024, 512, 1024
 FLOPS = 2 * K * H * S * 2 + 2 * H * H * M
@@ -57,6 +58,8 @@ def tile_list_shade_chart_scores_kernel(
         nc.gpsimd.memset(table_sc[:, 0, :].bitcast(I32), 0)
         nc.vector.memset(table_sc[:, 1, :].bitcast(I32), 0)
         nc.vector.memset(w2_raw_sc[:].rearrange("p a c -> p (a c)").bitcast(I32), 0)
+        identity = keep.tile([P, P], F32, name="identity")
+        make_identity(nc, identity[:])
         pages = []
         for n in range(TILES):
             pages.append(keep.tile([P, T2], F32, name=f"page{n}"))
@@ -75,8 +78,8 @@ def tile_list_shade_chart_scores_kernel(
         codes = {}
         scales = {}
 
-        def weave_weight(key, a, b, pool=ring):
-            staged[key, a, b] = pool.tile([P, PASS * PACK], BF16, name="staged", align_bytes=64)
+        def weave_weight(key, a, b):
+            staged[key, a, b] = ring.tile([P, PASS * PACK], BF16, name="staged", align_bytes=64)
             for part in range(2):
                 ms = slice(64 * part, 64 * (part + 1))
                 nc.scalar.activation(
@@ -86,8 +89,9 @@ def tile_list_shade_chart_scores_kernel(
                 )
 
         def quantise(key, a, b):
-            codes[key, a, b] = keep.tile([P, PASS], U32, name=f"codes_{key}{a}{b}", align_bytes=64)
-            scales[key, a, b] = keep.tile([P, PASS], U8, name=f"scales_{key}{a}{b}", align_bytes=64)
+            home = "w1" if b == 1 else key
+            codes[key, a, b] = keep.tile([P, PASS], U32, name=f"codes_{home}{a}{b}", align_bytes=64)
+            scales[key, a, b] = keep.tile([P, PASS], U8, name=f"scales_{home}{a}{b}", align_bytes=64)
             nc.vector.quantize_mx(
                 out=codes[key, a, b][:].bitcast(FP8X4), scales=scales[key, a, b][:], in_=staged[key, a, b][:]
             )
@@ -202,8 +206,8 @@ def tile_list_shade_chart_scores_kernel(
                     out=x_planes[b][:, i, ms], in_=reads[n][:, ms], func=ACT.Copy, scale=gv_sb[:, b, i : i + 1]
                 )
 
-        def weave_x(b, copy, pieces, pool=ring):
-            staged["x", b, 0] = pool.tile([P, M * PACK], BF16, name="staged", align_bytes=64)
+        def weave_x(b, copy, pieces):
+            staged["x", b, 0] = ring.tile([P, M * PACK], BF16, name="staged", align_bytes=64)
             for e in range(pieces):
                 cs = slice(M // 4 // pieces * e, M // 4 // pieces * (e + 1))
                 copy(
@@ -226,9 +230,13 @@ def tile_list_shade_chart_scores_kernel(
             if n == 4:
                 weave_x(0, nc.scalar.copy, 2)
                 quantise("x", 0, 0)
+            if n in (6, 7):
+                weave_weight("w4", n - 6, 1)
         pick(TILES - 1, 2)
-        weave_x(1, nc.vector.tensor_copy, 2, keep)
+        quantise("w4", 0, 1)
+        weave_x(1, nc.vector.tensor_copy, 2)
         quantise("x", 1, 0)
+        quantise("w4", 1, 1)
 
         out_rows = out.rearrange("(b p i) t -> b i p t", p=P, i=PACK)
         scores = []
@@ -246,31 +254,35 @@ def tile_list_shade_chart_scores_kernel(
                     start=(a == 0),
                     stop=(a == BLOCKS - 1),
                 )
-            gate = gm_sb[:, b, M * i : M * (i + 1)]
             gated = ring.tile([P, M], F32, name="size_b")
+            nc.vector.tensor_tensor(gated[:], bank[:], gm_sb[:, b, M * i : M * (i + 1)], ALU.mult)
+            scores.append(ring.tile([P, M], F32, name="score"))
             if n == 0:
-                engine = nc.vector
-                nc.vector.tensor_tensor(gated[:], bank[:], gate, ALU.mult)
-            else:
-                engine = nc.gpsimd
-                mixed = ring.tile([P, M], F32, name="top")
-                nc.scalar.copy(mixed[:], bank[:])
-                nc.gpsimd.tensor_tensor(gated[:], mixed[:], gate, ALU.mult)
-            score = ring.tile([P, M], F32, name="score")
-            engine.tensor_tensor(score[:], gated[:], reads[n][:], ALU.add)
-            scores.append(ring.tile([P, M], F32, name="weighted"))
-            engine.tensor_tensor(scores[n][:], score[:], wgo_sb[:], ALU.mult)
+                nc.vector.tensor_tensor(scores[n][:], gated[:], reads[n][:], ALU.add)
+                return
+            blocks = [slice(P * k, P * (k + 1)) for k in range(M // P)]
+            turned_sum = psum1.tile([P, M], F32, name="pb")
+            terms = [(term, cols) for term in (reads[n], gated) for cols in blocks]
+            for k, (term, cols) in enumerate(terms):
+                nc.tensor.matmul(
+                    turned_sum[:, cols], term[:, cols], identity[:],
+                    start=(k == 0), stop=(k == len(terms) - 1), is_transpose=True,
+                )
+            turned = ring.tile([P, M], F32, name="top")
+            nc.scalar.copy(turned[:], turned_sum[:])
+            upright = psum1.tile([P, M], F32, name="pa")
+            for cols in blocks:
+                nc.tensor.transpose(upright[:, cols], turned[:, cols], identity[:])
+            nc.scalar.copy(scores[n][:], upright[:])
 
         def file_scores(n):
             b, i = divmod(n, PACK)
-            nc.vector.tensor_copy(pages[n][:].indirect(list3[:]), scores[n][:])
+            nc.vector.tensor_tensor(pages[n][:].indirect(list3[:]), scores[n][:], wgo_sb[:], ALU.mult)
             nc.sync.dma_start(out_rows[b, i], pages[n][:])
 
         mix(0)
+        mix(1)
         for n in range(TILES):
-            if n < BLOCKS:
-                weave_weight("w4", n, 1, keep)
-                quantise("w4", n, 1)
-            if n + 1 < TILES:
-                mix(n + 1)
+            if n + 2 < TILES:
+                mix(n + 2)
             file_scores(n)

@@ -63,7 +63,7 @@ def tile_list_shade_chart_scores_kernel(
         pages = []
         for n in range(TILES):
             pages.append(keep.tile([P, T2], F32, name=f"page{n}"))
-            nc.vector.memset(pages[n][:].bitcast(I32), 0)
+            nc.gpsimd.memset(pages[n][:], 0.0)
 
         raw = {}
 
@@ -100,25 +100,26 @@ def tile_list_shade_chart_scores_kernel(
         nc.sync.dma_start(list2[:], offs2)
         nc.sync.dma_start(list3[:], offs3)
         nc.sync.dma_start(gv_sb[:], gv.rearrange("(b p i) -> p b i", p=P, i=PACK))
-        nc.sync.dma_start(wgt_sb[:], wgt)
         load_weight(w1, "w1", 0, 0, 4)
+        for a in range(PASSES):
+            nc.sync.dma_start(w2_raw[:, a, :].bitcast(I32), w2_words[a].bitcast(I32))
 
         def load_scale_rows(dst, src):
-            for q in range(4):
+            for r in range(4):
                 nc.sync.dma_start(
-                    dst[32 * q : 32 * q + 4].bitcast(I32),
-                    src[:, 4 * q : 4 * q + 4, :].rearrange("a q c -> q a c").bitcast(I32),
+                    dst[r:P:32].bitcast(I32),
+                    src.rearrange("a (q r) c -> r q a c", r=4)[r].bitcast(I32),
                 )
 
         def load_table(a):
             nc.sync.dma_start(table[a][:].bitcast(I32), tab_words[a].rearrange("p t i -> p (t i)").bitcast(I32))
 
         load_scale_rows(table_sc, tab_scales)
-        nc.sync.dma_start(w2_raw[:].bitcast(I32), w2_words.rearrange("a p c -> p a c").bitcast(I32))
         load_weight(w1, "w1", 1, 0)
         load_table(0)
         load_scale_rows(w2_raw_sc, w2_scales)
         load_table(1)
+        nc.sync.dma_start(wgt_sb[:], wgt)
         load_weight(w1, "w1", 0, 1)
         load_weight(w1, "w1", 1, 1)
 
@@ -254,11 +255,19 @@ def tile_list_shade_chart_scores_kernel(
                     start=(a == 0),
                     stop=(a == BLOCKS - 1),
                 )
-            gated = ring.tile([P, M], F32, name="size_b")
-            nc.vector.tensor_tensor(gated[:], bank[:], gm_sb[:, b, M * i : M * (i + 1)], ALU.mult)
-            scores.append(ring.tile([P, M], F32, name="score"))
+            gate = gm_sb[:, b, M * i : M * (i + 1)]
+            gated = ring.tile([P, M], F32, name="gated")
+            score = ring.tile([P, M], F32, name="score")
+            scores.append(ring.tile([P, M], F32, name="weighted"))
+            if n < 2:
+                nc.vector.tensor_tensor(gated[:], bank[:], gate, ALU.mult)
+            else:
+                mixed = ring.tile([P, M], F32, name="size_b")
+                nc.scalar.copy(mixed[:], bank[:])
+                nc.gpsimd.tensor_tensor(gated[:], mixed[:], gate, ALU.mult)
             if n == 0:
-                nc.vector.tensor_tensor(scores[n][:], gated[:], reads[n][:], ALU.add)
+                nc.vector.tensor_tensor(score[:], gated[:], reads[n][:], ALU.add)
+                nc.vector.tensor_tensor(scores[n][:], score[:], wgo_sb[:], ALU.mult)
                 return
             blocks = [slice(P * k, P * (k + 1)) for k in range(M // P)]
             turned_sum = psum1.tile([P, M], F32, name="pb")
@@ -273,11 +282,12 @@ def tile_list_shade_chart_scores_kernel(
             upright = psum1.tile([P, M], F32, name="pa")
             for cols in blocks:
                 nc.tensor.transpose(upright[:, cols], turned[:, cols], identity[:])
-            nc.scalar.copy(scores[n][:], upright[:])
+            nc.scalar.copy(score[:], upright[:])
+            nc.gpsimd.tensor_tensor(scores[n][:], score[:], wgo_sb[:], ALU.mult)
 
         def file_scores(n):
             b, i = divmod(n, PACK)
-            nc.vector.tensor_tensor(pages[n][:].indirect(list3[:]), scores[n][:], wgo_sb[:], ALU.mult)
+            nc.vector.tensor_copy(pages[n][:].indirect(list3[:]), scores[n][:])
             nc.sync.dma_start(out_rows[b, i], pages[n][:])
 
         mix(0)

@@ -37,8 +37,7 @@ def tile_list_shade_chart_scores_kernel(
         early = ctx.enter_context(tc.tile_pool(name="early", bufs=1))
         raws = ctx.enter_context(tc.tile_pool(name="raws", bufs=4))
         ring = ctx.enter_context(tc.tile_pool(name="ring", bufs=3))
-        psum1 = ctx.enter_context(tc.psum_pool(name="psum1", bufs=3))
-        psum2 = ctx.enter_context(tc.psum_pool(name="psum2", bufs=2))
+        psum1 = ctx.enter_context(tc.psum_pool(name="psum1", bufs=4))
 
         list1 = keep.tile([P, S // 16], U16, name="list1")
         list2 = keep.tile([P, M // 16], U16, name="list2")
@@ -81,20 +80,23 @@ def tile_list_shade_chart_scores_kernel(
         def weave_weight(key, a, b):
             staged[key, a, b] = ring.tile([P, PASS * PACK], BF16, name="staged", align_bytes=64)
             for part in range(2):
-                ms = slice(64 * part, 64 * (part + 1))
-                nc.scalar.activation(
-                    out=staged[key, a, b][:].rearrange("p (t m j) -> p m j t", t=PACK, j=PACK)[:, ms],
-                    in_=raw[key, a, b][:].rearrange("p j (m t) -> p m j t", t=PACK)[:, ms],
-                    func=ACT.Copy,
+                pairs = slice(32 * part, 32 * (part + 1))
+                nc.scalar.copy(
+                    out=staged[key, a, b][:].rearrange("p (t m e j) -> p m j e t", t=PACK, e=2, j=PACK)[:, pairs],
+                    in_=raw[key, a, b][:].rearrange("p j (m e t) -> p m j e t", e=2, t=PACK)[:, pairs],
                 )
 
-        def quantise(key, a, b):
+        def quantise(key, a, b, pieces=1):
             home = "w1" if b == 1 else key
             codes[key, a, b] = keep.tile([P, PASS], U32, name=f"codes_{home}{a}{b}", align_bytes=64)
             scales[key, a, b] = keep.tile([P, PASS], U8, name=f"scales_{home}{a}{b}", align_bytes=64)
-            nc.vector.quantize_mx(
-                out=codes[key, a, b][:].bitcast(FP8X4), scales=scales[key, a, b][:], in_=staged[key, a, b][:]
-            )
+            for e in range(pieces):
+                cols = slice(PASS // pieces * e, PASS // pieces * (e + 1))
+                nc.vector.quantize_mx(
+                    out=codes[key, a, b][:, cols].bitcast(FP8X4),
+                    scales=scales[key, a, b][:, cols],
+                    in_=staged[key, a, b][:, PACK * cols.start : PACK * cols.stop],
+                )
 
         nc.sync.dma_start(list1[:], offs)
         nc.sync.dma_start(list2[:], offs2)
@@ -184,7 +186,7 @@ def tile_list_shade_chart_scores_kernel(
                         start=(a == 0),
                         stop=(a == PASSES - 1),
                     )
-                size_b = ring.tile([P, BANK], F32, name="size_b")
+                size_b = ring.tile([P, BANK], F32, name="size_b", bufs=4)
                 nc.scalar.activation(out=size_b[:], in_=pb[:], func=ACT.Abs)
                 top = ring.tile([P, BANK], F32, name="top")
                 nc.vector.tensor_tensor(top[:], pa[:], size_b[:], ALU.max)
@@ -203,9 +205,14 @@ def tile_list_shade_chart_scores_kernel(
                 ms = slice(M // pieces * e, M // pieces * (e + 1))
                 entries = list2[:, M // 16 // pieces * e : M // 16 // pieces * (e + 1)]
                 nc.vector.tensor_tensor(reads[n][:, ms], h_tiles[n][:].indirect(entries), wgt_sb[:, ms], ALU.mult)
-                nc.scalar.activation(
-                    out=x_planes[b][:, i, ms], in_=reads[n][:, ms], func=ACT.Copy, scale=gv_sb[:, b, i : i + 1]
-                )
+                if n + 1 < TILES:
+                    nc.gpsimd.tensor_scalar(
+                        x_planes[b][:, i, ms], reads[n][:, ms], gv_sb[:, b, i : i + 1], 0.0, ALU.mult, ALU.add
+                    )
+                else:
+                    nc.scalar.activation(
+                        out=x_planes[b][:, i, ms], in_=reads[n][:, ms], func=ACT.Copy, scale=gv_sb[:, b, i : i + 1]
+                    )
 
         def weave_x(b, copy, pieces):
             staged["x", b, 0] = ring.tile([P, M * PACK], BF16, name="staged", align_bytes=64)
@@ -218,9 +225,9 @@ def tile_list_shade_chart_scores_kernel(
 
         for n in range(TILES):
             banks = products(n)
+            differences(n, banks)
             if n > 0:
                 pick(n - 1)
-            differences(n, banks)
             if n in (1, 2):
                 weave_weight("w1", n - 1, 1)
                 quantise("w1", n - 1, 1)
@@ -236,7 +243,7 @@ def tile_list_shade_chart_scores_kernel(
         pick(TILES - 1, 2)
         quantise("w4", 0, 1)
         weave_x(1, nc.vector.tensor_copy, 2)
-        quantise("x", 1, 0)
+        quantise("x", 1, 0, 2)
         quantise("w4", 1, 1)
 
         out_rows = out.rearrange("(b p i) t -> b i p t", p=P, i=PACK)
@@ -244,7 +251,7 @@ def tile_list_shade_chart_scores_kernel(
 
         def mix(n):
             b, i = divmod(n, PACK)
-            bank = psum2.tile([P, M], F32, name="mix")
+            bank = psum1.tile([P, M], F32, name="pa")
             for a in range(BLOCKS):
                 nc.tensor.matmul_mx(
                     out=bank[:],
@@ -262,7 +269,7 @@ def tile_list_shade_chart_scores_kernel(
             if n < 2:
                 nc.vector.tensor_tensor(gated[:], bank[:], gate, ALU.mult)
             else:
-                mixed = ring.tile([P, M], F32, name="size_b")
+                mixed = ring.tile([P, M], F32, name="size_b", bufs=4)
                 nc.scalar.copy(mixed[:], bank[:])
                 nc.gpsimd.tensor_tensor(gated[:], mixed[:], gate, ALU.mult)
             if n == 0:
@@ -279,7 +286,7 @@ def tile_list_shade_chart_scores_kernel(
                 )
             turned = ring.tile([P, M], F32, name="top")
             nc.scalar.copy(turned[:], turned_sum[:])
-            upright = psum1.tile([P, M], F32, name="pa")
+            upright = psum1.tile([P, M], F32, name="pb")
             for cols in blocks:
                 nc.tensor.transpose(upright[:, cols], turned[:, cols], identity[:])
             nc.scalar.copy(score[:], upright[:])

from contextlib import ExitStack

import concourse.mybir as mybir
from concourse.masks import make_identity

K, H, T, S, M, T2 = 1024, 1024, 4096, 1024, 512, 1024
FLOPS = 2 * K * H * S * 2 + 2 * H * H * M

F32 = mybir.dt.float32
BF16 = mybir.dt.bfloat16
I32 = mybir.dt.int32
U32 = mybir.dt.uint32
U16 = mybir.dt.uint16
U8 = mybir.dt.uint8
FP8X4 = mybir.dt.float8_e4m3fn_x4
FP4X4 = mybir.dt.float4_e2m1fn_x4
ALU = mybir.AluOpType
ACT = mybir.ActivationFunctionType

P = 128
PACK = 4
PASS = P * PACK
PASSES = K // PASS
BLOCKS = H // PASS
TILES = BLOCKS * PACK
BANK = 512
HALVES = S // BANK


def tile_list_shade_chart_scores_kernel(
    tc, tab_words, tab_scales, offs, offs2, offs3, w1, w2_words, w2_scales, gv, w4, gm, wgt, wgo, out
):
    nc = tc.nc
    with ExitStack() as ctx:
        keep = ctx.enter_context(tc.tile_pool(name="keep", bufs=1))
        shared = ctx.enter_context(tc.tile_pool(name="shared", bufs=1))
        early = ctx.enter_context(tc.tile_pool(name="early", bufs=1))
        raws = ctx.enter_context(tc.tile_pool(name="raws", bufs=4))
        ring = ctx.enter_context(tc.tile_pool(name="ring", bufs=3))
        psum1 = ctx.enter_context(tc.psum_pool(name="psum1", bufs=4))

        list1 = keep.tile([P, S // 16], U16, name="list1")
        list2 = keep.tile([P, M // 16], U16, name="list2")
        list3 = keep.tile([P, M // 16], U16, name="list3")

        table = [shared.tile([P, T], U32, name=f"table{a}", offset=4 * T * a) for a in range(PASSES)]
        table_sc = early.tile([P, PASSES, T], U8, name="table_sc", align_bytes=64, offset=0)
        w2_raw = keep.tile([P, PASSES, 2 * H], U8, name="w2_raw", align_bytes=64)
        w2_raw_sc = early.tile([P, PASSES, H], U8, name="w2_raw_sc", align_bytes=64, offset=PASSES * T)
        w2_q = keep.tile([P, PASSES, 2 * H], U8, name="w2_q", align_bytes=64)
        w2_sc = keep.tile([P, PASSES, H], U8, name="w2_sc", align_bytes=64)
        gv_sb = keep.tile([P, BLOCKS, PACK], F32, name="gv_sb")
        gm_sb = shared.tile([P, BLOCKS, PACK * M], F32, name="gm_sb", offset=0)
        wgt_sb = keep.tile([P, M], F32, name="wgt_sb")
        wgo_sb = keep.tile([P, M], F32, name="wgo_sb")

        nc.gpsimd.memset(table_sc[:, 0, :].bitcast(I32), 0)
        nc.vector.memset(table_sc[:, 1, :].bitcast(I32), 0)
        nc.vector.memset(w2_raw_sc[:].rearrange("p a c -> p (a c)").bitcast(I32), 0)
        identity = keep.tile([P, P], F32, name="identity")
        make_identity(nc, identity[:])
        pages = []
        for n in range(TILES):
            pages.append(keep.tile([P, T2], F32, name=f"page{n}"))
            nc.gpsimd.memset(pages[n][:], 0.0)

        raw = {}

        def load_weight(w, key, a, b, pieces=1):
            raw[key, a, b] = raws.tile([P, PACK, PASS], F32, name="raw")
            rows = w[PASS * a : PASS * (a + 1), PASS * b : PASS * (b + 1)].rearrange("(p j) c -> p j c", j=PACK)
            for e in range(pieces):
                js = slice(PACK // pieces * e, PACK // pieces * (e + 1))
                nc.sync.dma_start(raw[key, a, b][:, js, :], rows[:, js, :])

        staged = {}
        codes = {}
        scales = {}

        def weave_weight(key, a, b):
            staged[key, a, b] = ring.tile([P, PASS * PACK], BF16, name="staged", align_bytes=64)
            for part in range(2):
                pairs = slice(32 * part, 32 * (part + 1))
                nc.scalar.copy(
                    out=staged[key, a, b][:].rearrange("p (t m e j) -> p m j e t", t=PACK, e=2, j=PACK)[:, pairs],
                    in_=raw[key, a, b][:].rearrange("p j (m e t) -> p m j e t", e=2, t=PACK)[:, pairs],
                )

        def quantise(key, a, b, pieces=1):
            home = "w1" if b == 1 else key
            codes[key, a, b] = keep.tile([P, PASS], U32, name=f"codes_{home}{a}{b}", align_bytes=64)
            scales[key, a, b] = keep.tile([P, PASS], U8, name=f"scales_{home}{a}{b}", align_bytes=64)
            for e in range(pieces):
                cols = slice(PASS // pieces * e, PASS // pieces * (e + 1))
                nc.vector.quantize_mx(
                    out=codes[key, a, b][:, cols].bitcast(FP8X4),
                    scales=scales[key, a, b][:, cols],
                    in_=staged[key, a, b][:, PACK * cols.start : PACK * cols.stop],
                )

        nc.sync.dma_start(list1[:], offs)
        nc.sync.dma_start(list2[:], offs2)
        nc.sync.dma_start(list3[:], offs3)
        nc.sync.dma_start(gv_sb[:], gv.rearrange("(b p i) -> p b i", p=P, i=PACK))
        load_weight(w1, "w1", 0, 0, 4)
        for a in range(PASSES):
            nc.sync.dma_start(w2_raw[:, a, :].bitcast(I32), w2_words[a].bitcast(I32))

        def load_scale_rows(dst, src):
            for r in range(4):
                nc.sync.dma_start(
                    dst[r:P:32].bitcast(I32),
                    src.rearrange("a (q r) c -> r q a c", r=4)[r].bitcast(I32),
                )

        def load_table(a):
            nc.sync.dma_start(table[a][:].bitcast(I32), tab_words[a].rearrange("p t i -> p (t i)").bitcast(I32))

        load_scale_rows(table_sc, tab_scales)
        load_weight(w1, "w1", 1, 0)
        load_table(0)
        load_scale_rows(w2_raw_sc, w2_scales)
        load_table(1)
        nc.sync.dma_start(wgt_sb[:], wgt)
        load_weight(w1, "w1", 0, 1)
        load_weight(w1, "w1", 1, 1)

        for a in range(PASSES):
            weave_weight("w1", a, 0)
        load_weight(w4, "w4", 0, 0)
        load_weight(w4, "w4", 1, 0)

        v_sc = []
        for a in range(PASSES):
            v_sc.append(keep.tile([P, S], U8, name=f"v_sc{a}", align_bytes=64))
            nc.vector.tensor_copy(v_sc[a][:], table_sc[:, a, :].indirect(list1[:]))
        nc.vector.tensor_copy(
            out=w2_q[:].rearrange("p a c -> p (a c)").bitcast(U16).rearrange("p (g t m) -> p g t m", t=PACK, m=P),
            in_=w2_raw[:].rearrange("p a c -> p (a c)").bitcast(U16).rearrange("p (g m t) -> p g t m", t=PACK, m=P),
        )
        for a in range(PASSES):
            quantise("w1", a, 0)
        nc.vector.tensor_copy(
            out=w2_sc[:].rearrange("p a (b t m) -> p (a b) t m", t=PACK, m=P),
            in_=w2_raw_sc[:].rearrange("p a (b m t) -> p (a b) t m", t=PACK, m=P),
        )
        v_q = {}
        for a in range(PASSES):
            for c in range(HALVES):
                place = PASSES * T if (a, c) == (1, 0) else 4 * BANK * (HALVES * a + c)
                v_q[a, c] = early.tile([P, BANK], U32, name=f"v_q{a}{c}", align_bytes=64, offset=place)
                piece = list1[:, BANK // 16 * c : BANK // 16 * (c + 1)]
                nc.vector.tensor_copy(v_q[a, c][:], table[a][:].indirect(piece))

        nc.sync.dma_start(gm_sb[:], gm.rearrange("(b p i) m -> p b (i m)", p=P, i=PACK))
        nc.sync.dma_start(wgo_sb[:], wgo)

        reads = []
        x_planes = [keep.tile([P, PACK, M], BF16, name=f"x_planes{b}", align_bytes=64) for b in range(BLOCKS)]
        h_tiles = []

        def products(n):
            b, i = divmod(n, PACK)
            banks = []
            for c in range(HALVES):
                cols = slice(BANK * c, BANK * (c + 1))
                pb = psum1.tile([P, BANK], F32, name="pb")
                pa = psum1.tile([P, BANK], F32, name="pa")
                for a in range(PASSES):
                    nc.tensor.matmul_mx(
                        out=pb[:],
                        lhsT=w2_q[:, a, 2 * P * n : 2 * P * (n + 1)].bitcast(FP4X4),
                        lhsT_scale=w2_sc[:, a, P * n : P * (n + 1)],
                        rhs=v_q[a, c][:].bitcast(FP8X4),
                        rhs_scale=v_sc[a][:, cols],
                        start=(a == 0),
                        stop=(a == PASSES - 1),
                    )
                for a in range(PASSES):
                    nc.tensor.matmul_mx(
                        out=pa[:],
                        lhsT=codes["w1", a, b][:, P * i : P * (i + 1)].bitcast(FP8X4),
                        lhsT_scale=scales["w1", a, b][:, P * i : P * (i + 1)],
                        rhs=v_q[a, c][:].bitcast(FP8X4),
                        rhs_scale=v_sc[a][:, cols],
                        start=(a == 0),
                        stop=(a == PASSES - 1),
                    )
                size_b = ring.tile([P, BANK], F32, name="size_b", bufs=4)
                nc.scalar.activation(out=size_b[:], in_=pb[:], func=ACT.Abs)
                top = ring.tile([P, BANK], F32, name="top")
                nc.vector.tensor_tensor(top[:], pa[:], size_b[:], ALU.max)
                banks.append((top, pb))
            return banks

        def differences(n, banks):
            h_tiles.append(ring.tile([P, S], F32, name="h"))
            for c, (top, pb) in enumerate(banks):
                nc.vector.tensor_tensor(h_tiles[n][:, BANK * c : BANK * (c + 1)], top[:], pb[:], ALU.subtract)

        def pick(n, pieces=1):
            b, i = divmod(n, PACK)
            reads.append(keep.tile([P, M], F32, name=f"read{n}"))
            for e in range(pieces):
                ms = slice(M // pieces * e, M // pieces * (e + 1))
                entries = list2[:, M // 16 // pieces * e : M // 16 // pieces * (e + 1)]
                nc.vector.tensor_tensor(reads[n][:, ms], h_tiles[n][:].indirect(entries), wgt_sb[:, ms], ALU.mult)
                if n + 1 < TILES:
                    nc.gpsimd.tensor_scalar(
                        x_planes[b][:, i, ms], reads[n][:, ms], gv_sb[:, b, i : i + 1], 0.0, ALU.mult, ALU.add
                    )
                else:
                    nc.scalar.activation(
                        out=x_planes[b][:, i, ms], in_=reads[n][:, ms], func=ACT.Copy, scale=gv_sb[:, b, i : i + 1]
                    )

        def weave_x(b, copy, pieces):
            staged["x", b, 0] = ring.tile([P, M * PACK], BF16, name="staged", align_bytes=64)
            for e in range(pieces):
                cs = slice(M // 4 // pieces * e, M // 4 // pieces * (e + 1))
                copy(
                    out=staged["x", b, 0][:].rearrange("p (c e i) -> p c i e", e=4, i=PACK)[:, cs],
                    in_=x_planes[b][:].rearrange("p i (c e) -> p c i e", e=4)[:, cs],
                )

        for n in range(TILES):
            banks = products(n)
            differences(n, banks)
            if n > 0:
                pick(n - 1)
            if n in (1, 2):
                weave_weight("w1", n - 1, 1)
                quantise("w1", n - 1, 1)
                load_weight(w4, "w4", n - 1, 1)
            if n in (3, 5):
                weave_weight("w4", (n - 3) // 2, 0)
                quantise("w4", (n - 3) // 2, 0)
            if n == 4:
                weave_x(0, nc.scalar.copy, 2)
                quantise("x", 0, 0)
            if n in (6, 7):
                weave_weight("w4", n - 6, 1)
        pick(TILES - 1, 2)
        quantise("w4", 0, 1)
        weave_x(1, nc.vector.tensor_copy, 2)
        quantise("x", 1, 0, 2)
        quantise("w4", 1, 1)

        out_rows = out.rearrange("(b p i) t -> b i p t", p=P, i=PACK)
        scores = []

        def mix(n):
            b, i = divmod(n, PACK)
            bank = psum1.tile([P, M], F32, name="pa")
            for a in range(BLOCKS):
                nc.tensor.matmul_mx(
                    out=bank[:],
                    lhsT=codes["w4", a, b][:, P * i : P * (i + 1)].bitcast(FP8X4),
                    lhsT_scale=scales["w4", a, b][:, P * i : P * (i + 1)],
                    rhs=codes["x", a, 0][:].bitcast(FP8X4),
                    rhs_scale=scales["x", a, 0][:],
                    start=(a == 0),
                    stop=(a == BLOCKS - 1),
                )
            gate = gm_sb[:, b, M * i : M * (i + 1)]
            gated = ring.tile([P, M], F32, name="gated")
            score = ring.tile([P, M], F32, name="score")
            scores.append(ring.tile([P, M], F32, name="weighted"))
            if n < 2:
                nc.vector.tensor_tensor(gated[:], bank[:], gate, ALU.mult)
            else:
                mixed = ring.tile([P, M], F32, name="size_b", bufs=4)
                nc.scalar.copy(mixed[:], bank[:])
                nc.gpsimd.tensor_tensor(gated[:], mixed[:], gate, ALU.mult)
            if n == 0:
                nc.vector.tensor_tensor(score[:], gated[:], reads[n][:], ALU.add)
                nc.vector.tensor_tensor(scores[n][:], score[:], wgo_sb[:], ALU.mult)
                return
            blocks = [slice(P * k, P * (k + 1)) for k in range(M // P)]
            turned_sum = psum1.tile([P, M], F32, name="pb")
            terms = [(term, cols) for term in (reads[n], gated) for cols in blocks]
            for k, (term, cols) in enumerate(terms):
                nc.tensor.matmul(
                    turned_sum[:, cols], term[:, cols], identity[:],
                    start=(k == 0), stop=(k == len(terms) - 1), is_transpose=True,
                )
            turned = ring.tile([P, M], F32, name="top")
            nc.scalar.copy(turned[:], turned_sum[:])
            upright = psum1.tile([P, M], F32, name="pb")
            for cols in blocks:
                nc.tensor.transpose(upright[:, cols], turned[:, cols], identity[:])
            nc.scalar.copy(score[:], upright[:])
            nc.gpsimd.tensor_tensor(scores[n][:], score[:], wgo_sb[:], ALU.mult)

        def file_scores(n):
            b, i = divmod(n, PACK)
            nc.vector.tensor_copy(pages[n][:].indirect(list3[:]), scores[n][:])
            nc.sync.dma_start(out_rows[b, i], pages[n][:])

        mix(0)
        mix(1)
        for n in range(TILES):
            if n + 2 < TILES:
                mix(n + 2)
            file_scores(n)
